import numpy as np
import ml_dtypes


def mxq(x, axis, fmt="e4m3"):
    dtype, down = {"e4m3": (ml_dtypes.float8_e4m3fn, 7), "e5m2": (ml_dtypes.float8_e5m2, 14)}[fmt]
    v = np.moveaxis(np.asarray(x, np.float32).astype(ml_dtypes.bfloat16).astype(np.float64), axis, -1)
    blocks = v.reshape(v.shape[:-1] + (-1, 32))
    amax = np.abs(blocks).max(-1, keepdims=True)
    byte = np.maximum(np.where(amax > 0, np.frexp(amax)[1] - 1 + 127, 0) - down, 1)
    scale = np.exp2(byte - 127.0)
    codes = (blocks / scale).astype(np.float32).astype(dtype).astype(np.float64)
    return np.moveaxis((codes * scale).reshape(v.shape), -1, axis)


WIDE = False


def mx_kscale(k):
    if not WIDE:
        return np.ones(k)
    levels = np.array([10, -10, 5, -5, 0])
    if k % 512:
        return np.exp2(np.random.permutation(np.resize(levels, k // 32))).repeat(32)
    a = np.empty((k // 512, 16))
    for p in range(k // 512):
        a[p, :8] = np.random.permutation(np.resize(levels, 8))
        for g in range(8):
            far = levels[np.abs(levels - a[p, g]) >= 10]
            a[p, g + 8] = far[np.random.randint(len(far))]
    return np.exp2(a.ravel()).repeat(32)


def f64(x):
    return np.asarray(x).astype(np.float64)


def striped(idx):
    return np.tile(idx.reshape(-1, 16).T, (8, 1)).astype(np.uint16)


def unstriped(offs):
    return offs[:16].T.reshape(-1).astype(np.int64)


def pack_weight(w):
    k, n = w.shape
    w = f64(np.asarray(w, np.float32).astype(ml_dtypes.bfloat16)).reshape(k // 32, 32, n)
    amax = np.abs(w).max(1)
    byte = np.clip(np.where(amax > 0, np.frexp(amax)[1] - 1 + 127 - 7, 1), 1, 254)
    scaled = (w * np.exp2(127.0 - byte)[:, None, :]).reshape(k, n).astype(np.float32)
    words = np.ascontiguousarray(scaled.reshape(k // 512, 128, 4, n).transpose(0, 1, 3, 2)).astype(ml_dtypes.float8_e4m3fn).view(np.uint8)
    return words, np.ascontiguousarray(byte.astype(np.uint8).reshape(k // 512, 16, n))


def unpack_weight(words, scales):
    g, p, n, _ = words.shape
    vals = np.ascontiguousarray(words).view(ml_dtypes.float8_e4m3fn).astype(np.float64) * np.repeat(np.exp2(scales.astype(np.float64) - 127.0), 8, axis=1)[..., None]
    return vals.transpose(0, 1, 3, 2).reshape(g * 512, n)


K, T, E, C, N = 1024, 2048, 16, 256, 128


def by_expert(wq, xq):
    return np.concatenate([wq[e].T @ xq[:, e * C:(e + 1) * C] for e in range(E)], axis=1)


def setup_inputs():
    n = np.random.standard_normal
    s = mx_kscale(K)[:, None]
    first = np.random.permutation(np.repeat(np.arange(E), T // E))
    second = (first + 1 + np.random.permutation(np.repeat(np.arange(E - 1), -(-T // (E - 1)))[:T])) % E
    while np.bincount(second, minlength=E).max() != T // E:
        load = np.bincount(second, minlength=E); hi, lo = int(load.argmax()), int(load.argmin())
        t = np.flatnonzero((second == hi) & (first != lo))[0]; second[t] = lo
    slot_token = np.empty(E * C, np.int64); pos = np.empty((2, T), np.int64); fill = np.zeros(E, np.int64)
    place = np.stack([np.random.permutation(C) for _ in range(E)])
    for r, deal in enumerate((first, second)):
        for t in np.random.permutation(T):
            e = deal[t]; j = e * C + place[e, fill[e]]; fill[e] += 1; slot_token[j] = t; pos[r, t] = j
    g = np.random.uniform(0.2, 0.8, T)
    packed = [pack_weight(m) for m in n((E, K, N)) / np.sqrt(K) / s[None]]
    return {
        "xT": (n((K, T)) * s).astype(np.float32),
        "w_words": np.stack([m[0] for m in packed]),
        "w_scales": np.stack([m[1] for m in packed]),
        "gate": np.stack([np.tile(g, (N, 1)), np.tile(1.0 - g, (N, 1))]).astype(np.float32),
        "offs": striped(slot_token),
        "pos1": striped(pos[0]),
        "pos2": striped(pos[1]),
    }


def reference(xT, w_words, w_scales, gate, offs, pos1, pos2):
    idx = unstriped(offs)
    xq = mxq(f64(xT)[:, idx], 0, "e4m3")
    w = np.stack([unpack_weight(w_words[e], w_scales[e]) for e in range(E)])
    y = by_expert(w, xq)
    return f64(gate[0]) * y[:, unstriped(pos1)] + f64(gate[1]) * y[:, unstriped(pos2)]

@@ -1,0 +1,185 @@
+from contextlib import ExitStack
+
+import concourse.mybir as mybir
+from concourse.masks import make_identity
+
+K, T, E, C, N = 1024, 2048, 16, 256, 128
+FLOPS = 2 * K * N * E * C
+
+F32 = mybir.dt.float32
+BF16 = mybir.dt.bfloat16
+U32 = mybir.dt.uint32
+I32 = mybir.dt.int32
+U16 = mybir.dt.uint16
+U8 = mybir.dt.uint8
+FP8X4 = mybir.dt.float8_e4m3fn_x4
+MULT = mybir.AluOpType.mult
+ADD = mybir.AluOpType.add
+
+P = 128
+PASSES = K // 512
+S = E * C
+LOADS = (
+    ((0, 1024), (1024, 512), (1536, 256), (1792, 256)),
+    ((0, 512), (512, 512), (1024, 512), (1536, 256), (1792, 256)),
+)
+CHUNKS = (
+    ((0, 512, 304), (512, 512, 304), (1024, 512, 304), (1536, 256, 152), (1792, 256, 200)),
+    ((0, 512, 0), (512, 512, 0), (1024, 512, 0), (1536, 256, 0), (1792, 256, 0)),
+)
+
+
+def tile_routed_moe_kernel(tc, xT, w_words, w_scales, gate, offs, pos1, pos2, out):
+    nc = tc.nc
+    with ExitStack() as ctx:
+        lists = ctx.enter_context(tc.tile_pool(name="lists", bufs=1))
+        keep = ctx.enter_context(tc.tile_pool(name="keep", bufs=1))
+        stage = ctx.enter_context(tc.tile_pool(name="stage", bufs=4))
+        work = ctx.enter_context(tc.tile_pool(name="work", bufs=3))
+        outs = ctx.enter_context(tc.tile_pool(name="outs", bufs=5))
+        psum = ctx.enter_context(tc.psum_pool(name="psum", bufs=8))
+
+        offs_t = lists.tile([P, S // 16], U16, name="offs_t")
+        x_view = xT.rearrange("(a p j) t -> a p j t", p=P, j=4)
+        raw = {}
+        for a in range(PASSES):
+            for c, (t0, n) in enumerate(LOADS[a]):
+                r = keep.tile([P, 4, n], F32, name="raw%d_%d" % (a, c))
+                nc.sync.dma_start(out=r[:], in_=x_view[a, :, :, t0:t0 + n])
+                raw[(a, c)] = r
+                if a == 0 and c == 0:
+                    nc.sync.dma_start(offs_t[:], offs)
+
+        codes = [keep.tile([P, T], U32, name="codes%d" % a, align_bytes=64) for a in range(PASSES)]
+        sc = keep.tile([P, T], U8, name="sc", align_bytes=64)
+        gw = [keep.tile([P, S], U32, name="gw%d" % a, align_bytes=64) for a in range(PASSES)]
+        gb = keep.tile([P, S], U8, name="gb", align_bytes=64)
+        nc.vector.memset(sc[:].bitcast(I32), 0)
+
+        wsc = keep.tile([P, E * PASSES, N], U8, name="wsc", align_bytes=64)
+        nc.vector.memset(wsc[:].rearrange("p g n -> p (g n)").bitcast(I32), 0)
+        ws_view = w_scales.rearrange("e a (q r) n -> q r (e a) n", r=4)
+        for q in range(4):
+            nc.sync.dma_start(out=wsc[32 * q:32 * q + 4, :, :].bitcast(I32), in_=ws_view[q].bitcast(I32))
+        ww = keep.tile([P, E * PASSES, N], I32, name="ww", align_bytes=64)
+        ww_view = w_words.rearrange("e a p n r -> p (e a) (n r)").bitcast(I32)
+        for i in range(4):
+            nc.sync.dma_start(out=ww[:, 8 * i:8 * i + 8, :], in_=ww_view[:, 8 * i:8 * i + 8, :])
+
+        pos_t = []
+        for i, lst in enumerate((pos1, pos2)):
+            pt = lists.tile([P, T // 16], U16, name="pos_t%d" % i)
+            nc.sync.dma_start(pt[:], lst)
+            pos_t.append(pt)
+        gate_t = []
+        for i in range(2):
+            g = keep.tile([P, T], F32, name="gate_t%d" % i)
+            nc.sync.dma_start(out=g[:], in_=gate[i])
+            gate_t.append(g)
+
+        def interleave(a, c):
+            t0, n, v = CHUNKS[a][c]
+            grouped = stage.tile([P, 512, 4], BF16, name="grouped", align_bytes=64)
+            ld = [i for i, (l0, ln) in enumerate(LOADS[a]) if l0 <= t0 < l0 + ln][0]
+            src = raw[(a, ld)]
+            b = t0 - LOADS[a][ld][0]
+            if v > 0:
+                nc.vector.tensor_copy(
+                    out=grouped[:, 0:v, :].rearrange("p (c i) j -> p c j i", i=4),
+                    in_=src[:, :, b:b + v].rearrange("p j (c i) -> p c j i", i=4),
+                )
+            if v < n:
+                nc.scalar.copy(
+                    out=grouped[:, v:n, :].rearrange("p (c i) j -> p c j i", i=4),
+                    in_=src[:, :, b + v:b + n].rearrange("p j (c i) -> p c j i", i=4),
+                )
+            return grouped
+
+        def quantise(a, c, grouped):
+            t0, n, v = CHUNKS[a][c]
+            nc.vector.quantize_mx(
+                out=codes[a][:, t0:t0 + n].bitcast(FP8X4),
+                scales=sc[4 * a:P, t0:t0 + n],
+                in_=grouped[:, 0:n, :].rearrange("p w j -> p (w j)"),
+            )
+
+        def gather(dst, window, s0, s1):
+            nc.vector.tensor_copy(out=dst[:, s0:s1], in_=window[:].indirect(offs_t[:, s0 // 16:s1 // 16]))
+
+        for c in range(len(CHUNKS[0])):
+            quantise(0, c, interleave(0, c))
+        for s0, s1 in ((0, 1536), (1536, 3072), (3072, 4096)):
+            gather(gw[0], codes[0], s0, s1)
+        for c in range(len(CHUNKS[1])):
+            quantise(1, c, interleave(1, c))
+        for s0, s1 in ((0, 1536), (1536, 3072), (3072, 4096)):
+            gather(gb, sc, s0, s1)
+
+        y = keep.tile([P, S], F32, name="y")
+        ident = keep.tile([P, P], F32, name="ident")
+        make_identity(nc, ident[:])
+
+        def expert(e, acc, col):
+            for a in range(PASSES):
+                nc.tensor.matmul_mx(
+                    out=acc[:, col:col + C],
+                    lhsT=ww[:, PASSES * e + a, :].bitcast(FP8X4),
+                    lhsT_scale=wsc[:, PASSES * e + a, :],
+                    rhs=gw[a][:, e * C:(e + 1) * C].bitcast(FP8X4),
+                    rhs_scale=gb[4 * a:P, e * C:(e + 1) * C],
+                    start=(a == 0),
+                    stop=(a == PASSES - 1),
+                )
+
+        cuts = [0, 1536, 3072, 3840, 4096]
+        done = 0
+        for s0, s1 in zip(cuts[:-1], cuts[1:]):
+            gather(gw[1], codes[1], s0, s1)
+            while (done + 1) * C <= s1:
+                acc = psum.tile([P, 2 * C], F32, name="acc")
+                if done < E - 2:
+                    expert(done, acc, 0)
+                    expert(done + 1, acc, C)
+                    nc.scalar.copy(out=y[:, done * C:(done + 2) * C], in_=acc[:])
+                    done += 2
+                else:
+                    expert(done, acc, 0)
+                    if done < E - 1:
+                        nc.scalar.copy(out=y[:, done * C:(done + 1) * C], in_=acc[:, 0:C])
+                    else:
+                        nc.vector.tensor_copy(out=y[:, done * C:(done + 1) * C], in_=acc[:, 0:C])
+                    done += 1
+
+        def product(i, t0, t1):
+            m = work.tile([P, 512], F32, name="m%d" % i)
+            nc.vector.tensor_tensor(
+                out=m[:, 0:t1 - t0],
+                in0=y[:].indirect(pos_t[i][:, t0 // 16:t1 // 16]),
+                in1=gate_t[i][:, t0:t1],
+                op=MULT,
+            )
+            return m
+
+        def store(o, t0, t1):
+            nc.sync.dma_start(out=out[:, t0:t1], in_=o[:, 0:t1 - t0])
+
+        for t0 in (0, 512, 1024):
+            total = psum.tile([P, 512], F32, name="acc")
+            for i in range(2):
+                m = product(i, t0, t0 + 512)
+                nc.tensor.matmul(total[:], lhsT=ident[:], rhs=m[:], start=(i == 0), stop=(i == 1))
+            o = outs.tile([P, 512], F32, name="o")
+            nc.scalar.copy(out=o[:], in_=total[:])
+            store(o, t0, t0 + 512)
+
+        def vadd(ma, mb, t0, t1):
+            o = outs.tile([P, 512], F32, name="o")
+            nc.vector.tensor_tensor(out=o[:, 0:t1 - t0], in0=ma[:, 0:t1 - t0], in1=mb[:, 0:t1 - t0], op=ADD)
+            store(o, t0, t1)
+
+        a0 = product(0, 1536, 1792)
+        a1 = product(1, 1536, 1792)
+        b0 = product(0, 1792, 2048)
+        vadd(a0, a1, 1536, 1792)
+        b1 = product(1, 1792, 2048)
+        vadd(b0, b1, 1792, 2048)

@@ -19,6 +19,7 @@ ADD = mybir.AluOpType.add
 P = 128
 PASSES = K // 512
 S = E * C
+BANKS = 8
 LOADS = (
     ((0, 1024), (1024, 512), (1536, 256), (1792, 256)),
     ((0, 512), (512, 512), (1024, 512), (1536, 256), (1792, 256)),
@@ -119,36 +120,37 @@ def tile_routed_moe_kernel(tc, xT, w_words, w_scales, gate, offs, pos1, pos2, ou
         ident = keep.tile([P, P], F32, name="ident")
         make_identity(nc, ident[:])
 
-        def expert(e, acc, col):
-            for a in range(PASSES):
-                nc.tensor.matmul_mx(
-                    out=acc[:, col:col + C],
-                    lhsT=ww[:, PASSES * e + a, :].bitcast(FP8X4),
-                    lhsT_scale=wsc[:, PASSES * e + a, :],
-                    rhs=gw[a][:, e * C:(e + 1) * C].bitcast(FP8X4),
-                    rhs_scale=gb[4 * a:P, e * C:(e + 1) * C],
-                    start=(a == 0),
-                    stop=(a == PASSES - 1),
-                )
+        accs = {}
 
-        cuts = [0, 1536, 3072, 3840, 4096]
-        done = 0
+        def mx_pass(e, a):
+            nc.tensor.matmul_mx(
+                out=accs[e][:, 0:C],
+                lhsT=ww[:, PASSES * e + a, :].bitcast(FP8X4),
+                lhsT_scale=wsc[:, PASSES * e + a, :],
+                rhs=gw[a][:, e * C:(e + 1) * C].bitcast(FP8X4),
+                rhs_scale=gb[4 * a:P, e * C:(e + 1) * C],
+                start=(a == 0),
+                stop=(a == PASSES - 1),
+            )
+
+        def open_group(e):
+            acc = psum.tile([P, 2 * C], F32, name="acc")
+            accs[e] = acc
+            mx_pass(e, 0)
+
+        for e in range(BANKS):
+            open_group(e)
+        cuts = [0, 1536, 2560, 3328, 3840, 4096]
         for s0, s1 in zip(cuts[:-1], cuts[1:]):
             gather(gw[1], codes[1], s0, s1)
-            while (done + 1) * C <= s1:
-                acc = psum.tile([P, 2 * C], F32, name="acc")
-                if done < E - 2:
-                    expert(done, acc, 0)
-                    expert(done + 1, acc, C)
-                    nc.scalar.copy(out=y[:, done * C:(done + 2) * C], in_=acc[:])
-                    done += 2
+            for e in range(s0 // C, s1 // C):
+                mx_pass(e, 1)
+                if e < E - 1:
+                    nc.scalar.copy(out=y[:, e * C:(e + 1) * C], in_=accs[e][:, 0:C])
                 else:
-                    expert(done, acc, 0)
-                    if done < E - 1:
-                        nc.scalar.copy(out=y[:, done * C:(done + 1) * C], in_=acc[:, 0:C])
-                    else:
-                        nc.vector.tensor_copy(out=y[:, done * C:(done + 1) * C], in_=acc[:, 0:C])
-                    done += 1
+                    nc.vector.tensor_copy(out=y[:, e * C:(e + 1) * C], in_=accs[e][:, 0:C])
+            for e in range(s0 // C + BANKS, min(s1 // C + BANKS, E)):
+                open_group(e)
 
         def product(i, t0, t1):
             m = work.tile([P, 512], F32, name="m%d" % i)

@@ -37,7 +37,7 @@ def tile_routed_moe_kernel(tc, xT, w_words, w_scales, gate, offs, pos1, pos2, ou
         keep = ctx.enter_context(tc.tile_pool(name="keep", bufs=1))
         stage = ctx.enter_context(tc.tile_pool(name="stage", bufs=4))
         work = ctx.enter_context(tc.tile_pool(name="work", bufs=3))
-        outs = ctx.enter_context(tc.tile_pool(name="outs", bufs=5))
+        outs = ctx.enter_context(tc.tile_pool(name="outs", bufs=6))
         psum = ctx.enter_context(tc.psum_pool(name="psum", bufs=8))
 
         offs_t = lists.tile([P, S // 16], U16, name="offs_t")
@@ -165,14 +165,15 @@ def tile_routed_moe_kernel(tc, xT, w_words, w_scales, gate, offs, pos1, pos2, ou
         def store(o, t0, t1):
             nc.sync.dma_start(out=out[:, t0:t1], in_=o[:, 0:t1 - t0])
 
-        for t0 in (0, 512, 1024):
+        for t0, t1 in ((0, 128), (128, 512), (512, 1024), (1024, 1536)):
+            n = t1 - t0
             total = psum.tile([P, 512], F32, name="acc")
             for i in range(2):
-                m = product(i, t0, t0 + 512)
-                nc.tensor.matmul(total[:], lhsT=ident[:], rhs=m[:], start=(i == 0), stop=(i == 1))
+                m = product(i, t0, t1)
+                nc.tensor.matmul(total[:, 0:n], lhsT=ident[:], rhs=m[:, 0:n], start=(i == 0), stop=(i == 1))
             o = outs.tile([P, 512], F32, name="o")
-            nc.scalar.copy(out=o[:], in_=total[:])
-            store(o, t0, t0 + 512)
+            nc.scalar.copy(out=o[:, 0:n], in_=total[:, 0:n])
+            store(o, t0, t1)
 
         def vadd(ma, mb, t0, t1):
             o = outs.tile([P, 512], F32, name="o")

@@ -165,7 +165,7 @@ def tile_routed_moe_kernel(tc, xT, w_words, w_scales, gate, offs, pos1, pos2, ou
         def store(o, t0, t1):
             nc.sync.dma_start(out=out[:, t0:t1], in_=o[:, 0:t1 - t0])
 
-        for t0, t1 in ((0, 128), (128, 512), (512, 1024), (1024, 1536)):
+        for t0, t1 in ((0, 128), (128, 608), (608, 1120), (1120, 1632)):
             n = t1 - t0
             total = psum.tile([P, 512], F32, name="acc")
             for i in range(2):
@@ -180,9 +180,9 @@ def tile_routed_moe_kernel(tc, xT, w_words, w_scales, gate, offs, pos1, pos2, ou
             nc.vector.tensor_tensor(out=o[:, 0:t1 - t0], in0=ma[:, 0:t1 - t0], in1=mb[:, 0:t1 - t0], op=ADD)
             store(o, t0, t1)
 
-        a0 = product(0, 1536, 1792)
-        a1 = product(1, 1536, 1792)
-        b0 = product(0, 1792, 2048)
-        vadd(a0, a1, 1536, 1792)
-        b1 = product(1, 1792, 2048)
-        vadd(b0, b1, 1792, 2048)
+        a0 = product(0, 1632, 1920)
+        a1 = product(1, 1632, 1920)
+        b0 = product(0, 1920, 2048)
+        vadd(a0, a1, 1632, 1920)
+        b1 = product(1, 1920, 2048)
+        vadd(b0, b1, 1920, 2048)

@@ -35,7 +35,7 @@ def tile_routed_moe_kernel(tc, xT, w_words, w_scales, gate, offs, pos1, pos2, ou
     with ExitStack() as ctx:
         lists = ctx.enter_context(tc.tile_pool(name="lists", bufs=1))
         keep = ctx.enter_context(tc.tile_pool(name="keep", bufs=1))
-        stage = ctx.enter_context(tc.tile_pool(name="stage", bufs=4))
+        stage = ctx.enter_context(tc.tile_pool(name="stage", bufs=6))
         work = ctx.enter_context(tc.tile_pool(name="work", bufs=3))
         outs = ctx.enter_context(tc.tile_pool(name="outs", bufs=6))
         psum = ctx.enter_context(tc.psum_pool(name="psum", bufs=8))

@@ -165,7 +165,7 @@ def tile_routed_moe_kernel(tc, xT, w_words, w_scales, gate, offs, pos1, pos2, ou
         def store(o, t0, t1):
             nc.sync.dma_start(out=out[:, t0:t1], in_=o[:, 0:t1 - t0])
 
-        for t0, t1 in ((0, 128), (128, 608), (608, 1120), (1120, 1632)):
+        for t0, t1 in ((0, 128), (128, 544), (544, 1056), (1056, 1568)):
             n = t1 - t0
             total = psum.tile([P, 512], F32, name="acc")
             for i in range(2):
@@ -180,9 +180,9 @@ def tile_routed_moe_kernel(tc, xT, w_words, w_scales, gate, offs, pos1, pos2, ou
             nc.vector.tensor_tensor(out=o[:, 0:t1 - t0], in0=ma[:, 0:t1 - t0], in1=mb[:, 0:t1 - t0], op=ADD)
             store(o, t0, t1)
 
-        a0 = product(0, 1632, 1920)
-        a1 = product(1, 1632, 1920)
+        a0 = product(0, 1568, 1920)
+        a1 = product(1, 1568, 1920)
         b0 = product(0, 1920, 2048)
-        vadd(a0, a1, 1632, 1920)
+        vadd(a0, a1, 1568, 1920)
         b1 = product(1, 1920, 2048)
         vadd(b0, b1, 1920, 2048)

@@ -21,11 +21,11 @@ PASSES = K // 512
 S = E * C
 BANKS = 8
 LOADS = (
-    ((0, 1024), (1024, 512), (1536, 256), (1792, 256)),
+    ((0, 1024), (1024, 512), (1536, 256), (1792, 128), (1920, 128)),
     ((0, 512), (512, 512), (1024, 512), (1536, 256), (1792, 256)),
 )
 CHUNKS = (
-    ((0, 512, 304), (512, 512, 304), (1024, 512, 304), (1536, 256, 152), (1792, 256, 200)),
+    ((0, 512, 304), (512, 512, 304), (1024, 512, 304), (1536, 256, 152), (1792, 128, 80), (1920, 128, 104)),
     ((0, 512, 0), (512, 512, 0), (1024, 512, 0), (1536, 256, 0), (1792, 256, 0)),
 )
 

@@ -145,7 +145,7 @@ def tile_routed_moe_kernel(tc, xT, w_words, w_scales, gate, offs, pos1, pos2, ou
             gather(gw[1], codes[1], s0, s1)
             for e in range(s0 // C, s1 // C):
                 mx_pass(e, 1)
-                if e < E - 1:
+                if e < E - 2:
                     nc.scalar.copy(out=y[:, e * C:(e + 1) * C], in_=accs[e][:, 0:C])
                 else:
                     nc.vector.tensor_copy(out=y[:, e * C:(e + 1) * C], in_=accs[e][:, 0:C])

@@ -22,11 +22,11 @@ S = E * C
 BANKS = 8
 LOADS = (
     ((0, 1024), (1024, 512), (1536, 256), (1792, 128), (1920, 128)),
-    ((0, 512), (512, 512), (1024, 512), (1536, 256), (1792, 256)),
+    ((0, 256), (256, 512), (768, 512), (1280, 512), (1792, 256)),
 )
 CHUNKS = (
     ((0, 512, 304), (512, 512, 304), (1024, 512, 304), (1536, 256, 152), (1792, 128, 80), (1920, 128, 104)),
-    ((0, 512, 0), (512, 512, 0), (1024, 512, 0), (1536, 256, 0), (1792, 256, 0)),
+    ((0, 256, 0), (256, 512, 0), (768, 512, 0), (1280, 512, 0), (1792, 256, 0)),
 )
 
 

@@ -21,11 +21,11 @@ PASSES = K // 512
 S = E * C
 BANKS = 8
 LOADS = (
-    ((0, 1024), (1024, 512), (1536, 256), (1792, 128), (1920, 128)),
+    ((0, 512), (512, 512), (1024, 512), (1536, 256), (1792, 128), (1920, 128)),
     ((0, 256), (256, 512), (768, 512), (1280, 512), (1792, 256)),
 )
 CHUNKS = (
-    ((0, 512, 304), (512, 512, 304), (1024, 512, 304), (1536, 256, 152), (1792, 128, 80), (1920, 128, 104)),
+    ((0, 512, 256), (512, 512, 256), (1024, 512, 256), (1536, 256, 128), (1792, 128, 64), (1920, 128, 80)),
     ((0, 256, 0), (256, 512, 0), (768, 512, 0), (1280, 512, 0), (1792, 256, 0)),
 )
 

@@ -120,37 +120,43 @@ def tile_routed_moe_kernel(tc, xT, w_words, w_scales, gate, offs, pos1, pos2, ou
         ident = keep.tile([P, P], F32, name="ident")
         make_identity(nc, ident[:])
 
+        GROUPS = [(e * C, C) for e in range(E - 1)] + [(S - C, C // 2), (S - C // 2, C // 2)]
         accs = {}
 
-        def mx_pass(e, a):
+        def mx_pass(g, a):
+            s0, n = GROUPS[g]
+            e = s0 // C
             nc.tensor.matmul_mx(
-                out=accs[e][:, 0:C],
+                out=accs[g][:, 0:n],
                 lhsT=ww[:, PASSES * e + a, :].bitcast(FP8X4),
                 lhsT_scale=wsc[:, PASSES * e + a, :],
-                rhs=gw[a][:, e * C:(e + 1) * C].bitcast(FP8X4),
-                rhs_scale=gb[4 * a:P, e * C:(e + 1) * C],
+                rhs=gw[a][:, s0:s0 + n].bitcast(FP8X4),
+                rhs_scale=gb[4 * a:P, s0:s0 + n],
                 start=(a == 0),
                 stop=(a == PASSES - 1),
             )
 
-        def open_group(e):
+        def open_group(g):
             acc = psum.tile([P, 2 * C], F32, name="acc")
-            accs[e] = acc
-            mx_pass(e, 0)
+            accs[g] = acc
+            mx_pass(g, 0)
 
-        for e in range(BANKS):
-            open_group(e)
+        for g in range(BANKS):
+            open_group(g)
         cuts = [0, 1536, 2560, 3328, 3840, 4096]
         for s0, s1 in zip(cuts[:-1], cuts[1:]):
             gather(gw[1], codes[1], s0, s1)
-            for e in range(s0 // C, s1 // C):
-                mx_pass(e, 1)
-                if e < E - 2:
-                    nc.scalar.copy(out=y[:, e * C:(e + 1) * C], in_=accs[e][:, 0:C])
+            done = [g for g, (g0, n) in enumerate(GROUPS) if s0 <= g0 < s1]
+            for g in done:
+                mx_pass(g, 1)
+                g0, n = GROUPS[g]
+                if g in (E - 2, E):
+                    nc.vector.tensor_copy(out=y[:, g0:g0 + n], in_=accs[g][:, 0:n])
                 else:
-                    nc.vector.tensor_copy(out=y[:, e * C:(e + 1) * C], in_=accs[e][:, 0:C])
-            for e in range(s0 // C + BANKS, min(s1 // C + BANKS, E)):
-                open_group(e)
+                    nc.scalar.copy(out=y[:, g0:g0 + n], in_=accs[g][:, 0:n])
+            for g in done:
+                if g + BANKS < len(GROUPS):
+                    open_group(g + BANKS)
 
         def product(i, t0, t1):
             m = work.tile([P, 512], F32, name="m%d" % i)

@@ -36,8 +36,8 @@ def tile_routed_moe_kernel(tc, xT, w_words, w_scales, gate, offs, pos1, pos2, ou
         lists = ctx.enter_context(tc.tile_pool(name="lists", bufs=1))
         keep = ctx.enter_context(tc.tile_pool(name="keep", bufs=1))
         stage = ctx.enter_context(tc.tile_pool(name="stage", bufs=6))
-        work = ctx.enter_context(tc.tile_pool(name="work", bufs=3))
-        outs = ctx.enter_context(tc.tile_pool(name="outs", bufs=6))
+        work = ctx.enter_context(tc.tile_pool(name="work", bufs=1))
+        outs = ctx.enter_context(tc.tile_pool(name="outs", bufs=1))
         psum = ctx.enter_context(tc.psum_pool(name="psum", bufs=8))
 
         offs_t = lists.tile([P, S // 16], U16, name="offs_t")
@@ -159,7 +159,7 @@ def tile_routed_moe_kernel(tc, xT, w_words, w_scales, gate, offs, pos1, pos2, ou
                     open_group(g + BANKS)
 
         def product(i, t0, t1):
-            m = work.tile([P, 512], F32, name="m%d" % i)
+            m = work.tile([P, t1 - t0], F32, name="m%d_%d" % (i, t0))
             nc.vector.tensor_tensor(
                 out=m[:, 0:t1 - t0],
                 in0=y[:].indirect(pos_t[i][:, t0 // 16:t1 // 16]),
@@ -171,24 +171,31 @@ def tile_routed_moe_kernel(tc, xT, w_words, w_scales, gate, offs, pos1, pos2, ou
         def store(o, t0, t1):
             nc.sync.dma_start(out=out[:, t0:t1], in_=o[:, 0:t1 - t0])
 
-        for t0, t1 in ((0, 128), (128, 544), (544, 1056), (1056, 1568)):
-            n = t1 - t0
-            total = psum.tile([P, 512], F32, name="acc")
-            for i in range(2):
-                m = product(i, t0, t1)
-                nc.tensor.matmul(total[:, 0:n], lhsT=ident[:], rhs=m[:, 0:n], start=(i == 0), stop=(i == 1))
-            o = outs.tile([P, 512], F32, name="o")
-            nc.scalar.copy(out=o[:, 0:n], in_=total[:, 0:n])
-            store(o, t0, t1)
+        for t0, t1, step in ((0, 128, 128), (128, 640, 512), (640, 1248, 304)):
+            m0 = product(0, t0, t1)
+            m1 = product(1, t0, t1)
+            for c0 in range(t0, t1, step):
+                total = psum.tile([P, 512], F32, name="acc")
+                for i, m in enumerate((m0, m1)):
+                    nc.tensor.matmul(
+                        total[:, 0:step],
+                        lhsT=ident[:],
+                        rhs=m[:, c0 - t0:c0 - t0 + step],
+                        start=(i == 0),
+                        stop=(i == 1),
+                    )
+                o = outs.tile([P, step], F32, name="o%d" % c0)
+                nc.scalar.copy(out=o[:], in_=total[:, 0:step])
+                store(o, c0, c0 + step)
 
         def vadd(ma, mb, t0, t1):
-            o = outs.tile([P, 512], F32, name="o")
+            o = outs.tile([P, t1 - t0], F32, name="o%d" % t0)
             nc.vector.tensor_tensor(out=o[:, 0:t1 - t0], in0=ma[:, 0:t1 - t0], in1=mb[:, 0:t1 - t0], op=ADD)
             store(o, t0, t1)
 
-        a0 = product(0, 1568, 1920)
-        a1 = product(1, 1568, 1920)
+        a0 = product(0, 1248, 1920)
+        a1 = product(1, 1248, 1920)
         b0 = product(0, 1920, 2048)
-        vadd(a0, a1, 1568, 1920)
+        vadd(a0, a1, 1248, 1920)
         b1 = product(1, 1920, 2048)
         vadd(b0, b1, 1920, 2048)

@@ -150,7 +150,7 @@ def tile_routed_moe_kernel(tc, xT, w_words, w_scales, gate, offs, pos1, pos2, ou
             for g in done:
                 mx_pass(g, 1)
                 g0, n = GROUPS[g]
-                if g in (E - 2, E):
+                if g in (E - 2, E - 1):
                     nc.vector.tensor_copy(out=y[:, g0:g0 + n], in_=accs[g][:, 0:n])
                 else:
                     nc.scalar.copy(out=y[:, g0:g0 + n], in_=accs[g][:, 0:n])
@@ -171,10 +171,11 @@ def tile_routed_moe_kernel(tc, xT, w_words, w_scales, gate, offs, pos1, pos2, ou
         def store(o, t0, t1):
             nc.sync.dma_start(out=out[:, t0:t1], in_=o[:, 0:t1 - t0])
 
-        for t0, t1, step in ((0, 128, 128), (128, 640, 512), (640, 1248, 304)):
+        for t0, t1, sums in ((0, 128, (128,)), (128, 640, (512,)), (640, 1216, (320, 256))):
             m0 = product(0, t0, t1)
             m1 = product(1, t0, t1)
-            for c0 in range(t0, t1, step):
+            c0 = t0
+            for step in sums:
                 total = psum.tile([P, 512], F32, name="acc")
                 for i, m in enumerate((m0, m1)):
                     nc.tensor.matmul(
@@ -187,15 +188,16 @@ def tile_routed_moe_kernel(tc, xT, w_words, w_scales, gate, offs, pos1, pos2, ou
                 o = outs.tile([P, step], F32, name="o%d" % c0)
                 nc.scalar.copy(out=o[:], in_=total[:, 0:step])
                 store(o, c0, c0 + step)
+                c0 += step
 
         def vadd(ma, mb, t0, t1):
             o = outs.tile([P, t1 - t0], F32, name="o%d" % t0)
             nc.vector.tensor_tensor(out=o[:, 0:t1 - t0], in0=ma[:, 0:t1 - t0], in1=mb[:, 0:t1 - t0], op=ADD)
             store(o, t0, t1)
 
-        a0 = product(0, 1248, 1920)
-        a1 = product(1, 1248, 1920)
+        a0 = product(0, 1216, 1920)
+        a1 = product(1, 1216, 1920)
         b0 = product(0, 1920, 2048)
-        vadd(a0, a1, 1248, 1920)
+        vadd(a0, a1, 1216, 1920)
         b1 = product(1, 1920, 2048)
         vadd(b0, b1, 1920, 2048)

from contextlib import ExitStack

import concourse.mybir as mybir
from concourse.masks import make_identity

K, T, E, C, N = 1024, 2048, 16, 256, 128
FLOPS = 2 * K * N * E * C

F32 = mybir.dt.float32
BF16 = mybir.dt.bfloat16
U32 = mybir.dt.uint32
I32 = mybir.dt.int32
U16 = mybir.dt.uint16
U8 = mybir.dt.uint8
FP8X4 = mybir.dt.float8_e4m3fn_x4
MULT = mybir.AluOpType.mult
ADD = mybir.AluOpType.add

P = 128
PASSES = K // 512
S = E * C
BANKS = 8
LOADS = (
    ((0, 512), (512, 512), (1024, 512), (1536, 256), (1792, 128), (1920, 128)),
    ((0, 256), (256, 512), (768, 512), (1280, 512), (1792, 256)),
)
CHUNKS = (
    ((0, 512, 256), (512, 512, 256), (1024, 512, 256), (1536, 256, 128), (1792, 128, 64), (1920, 128, 80)),
    ((0, 256, 0), (256, 512, 0), (768, 512, 0), (1280, 512, 0), (1792, 256, 0)),
)


def tile_routed_moe_kernel(tc, xT, w_words, w_scales, gate, offs, pos1, pos2, out):
    nc = tc.nc
    with ExitStack() as ctx:
        lists = ctx.enter_context(tc.tile_pool(name="lists", bufs=1))
        keep = ctx.enter_context(tc.tile_pool(name="keep", bufs=1))
        stage = ctx.enter_context(tc.tile_pool(name="stage", bufs=6))
        work = ctx.enter_context(tc.tile_pool(name="work", bufs=1))
        outs = ctx.enter_context(tc.tile_pool(name="outs", bufs=1))
        psum = ctx.enter_context(tc.psum_pool(name="psum", bufs=8))

        offs_t = lists.tile([P, S // 16], U16, name="offs_t")
        x_view = xT.rearrange("(a p j) t -> a p j t", p=P, j=4)
        raw = {}
        for a in range(PASSES):
            for c, (t0, n) in enumerate(LOADS[a]):
                r = keep.tile([P, 4, n], F32, name="raw%d_%d" % (a, c))
                nc.sync.dma_start(out=r[:], in_=x_view[a, :, :, t0:t0 + n])
                raw[(a, c)] = r
                if a == 0 and c == 0:
                    nc.sync.dma_start(offs_t[:], offs)

        codes = [keep.tile([P, T], U32, name="codes%d" % a, align_bytes=64) for a in range(PASSES)]
        sc = keep.tile([P, T], U8, name="sc", align_bytes=64)
        gw = [keep.tile([P, S], U32, name="gw%d" % a, align_bytes=64) for a in range(PASSES)]
        gb = keep.tile([P, S], U8, name="gb", align_bytes=64)
        nc.vector.memset(sc[:].bitcast(I32), 0)

        wsc = keep.tile([P, E * PASSES, N], U8, name="wsc", align_bytes=64)
        nc.vector.memset(wsc[:].rearrange("p g n -> p (g n)").bitcast(I32), 0)
        ws_view = w_scales.rearrange("e a (q r) n -> q r (e a) n", r=4)
        for q in range(4):
            nc.sync.dma_start(out=wsc[32 * q:32 * q + 4, :, :].bitcast(I32), in_=ws_view[q].bitcast(I32))
        ww = keep.tile([P, E * PASSES, N], I32, name="ww", align_bytes=64)
        ww_view = w_words.rearrange("e a p n r -> p (e a) (n r)").bitcast(I32)
        for i in range(4):
            nc.sync.dma_start(out=ww[:, 8 * i:8 * i + 8, :], in_=ww_view[:, 8 * i:8 * i + 8, :])

        pos_t = []
        for i, lst in enumerate((pos1, pos2)):
            pt = lists.tile([P, T // 16], U16, name="pos_t%d" % i)
            nc.sync.dma_start(pt[:], lst)
            pos_t.append(pt)
        gate_t = []
        for i in range(2):
            g = keep.tile([P, T], F32, name="gate_t%d" % i)
            nc.sync.dma_start(out=g[:], in_=gate[i])
            gate_t.append(g)

        def interleave(a, c):
            t0, n, v = CHUNKS[a][c]
            grouped = stage.tile([P, 512, 4], BF16, name="grouped", align_bytes=64)
            ld = [i for i, (l0, ln) in enumerate(LOADS[a]) if l0 <= t0 < l0 + ln][0]
            src = raw[(a, ld)]
            b = t0 - LOADS[a][ld][0]
            if v > 0:
                nc.vector.tensor_copy(
                    out=grouped[:, 0:v, :].rearrange("p (c i) j -> p c j i", i=4),
                    in_=src[:, :, b:b + v].rearrange("p j (c i) -> p c j i", i=4),
                )
            if v < n:
                nc.scalar.copy(
                    out=grouped[:, v:n, :].rearrange("p (c i) j -> p c j i", i=4),
                    in_=src[:, :, b + v:b + n].rearrange("p j (c i) -> p c j i", i=4),
                )
            return grouped

        def quantise(a, c, grouped):
            t0, n, v = CHUNKS[a][c]
            nc.vector.quantize_mx(
                out=codes[a][:, t0:t0 + n].bitcast(FP8X4),
                scales=sc[4 * a:P, t0:t0 + n],
                in_=grouped[:, 0:n, :].rearrange("p w j -> p (w j)"),
            )

        def gather(dst, window, s0, s1):
            nc.vector.tensor_copy(out=dst[:, s0:s1], in_=window[:].indirect(offs_t[:, s0 // 16:s1 // 16]))

        for c in range(len(CHUNKS[0])):
            quantise(0, c, interleave(0, c))
        for s0, s1 in ((0, 1536), (1536, 3072), (3072, 4096)):
            gather(gw[0], codes[0], s0, s1)
        for c in range(len(CHUNKS[1])):
            quantise(1, c, interleave(1, c))
        for s0, s1 in ((0, 1536), (1536, 3072), (3072, 4096)):
            gather(gb, sc, s0, s1)

        y = keep.tile([P, S], F32, name="y")
        ident = keep.tile([P, P], F32, name="ident")
        make_identity(nc, ident[:])

        GROUPS = [(e * C, C) for e in range(E - 1)] + [(S - C, C // 2), (S - C // 2, C // 2)]
        accs = {}

        def mx_pass(g, a):
            s0, n = GROUPS[g]
            e = s0 // C
            nc.tensor.matmul_mx(
                out=accs[g][:, 0:n],
                lhsT=ww[:, PASSES * e + a, :].bitcast(FP8X4),
                lhsT_scale=wsc[:, PASSES * e + a, :],
                rhs=gw[a][:, s0:s0 + n].bitcast(FP8X4),
                rhs_scale=gb[4 * a:P, s0:s0 + n],
                start=(a == 0),
                stop=(a == PASSES - 1),
            )

        def open_group(g):
            acc = psum.tile([P, 2 * C], F32, name="acc")
            accs[g] = acc
            mx_pass(g, 0)

        for g in range(BANKS):
            open_group(g)
        cuts = [0, 1536, 2560, 3328, 3840, 4096]
        for s0, s1 in zip(cuts[:-1], cuts[1:]):
            gather(gw[1], codes[1], s0, s1)
            done = [g for g, (g0, n) in enumerate(GROUPS) if s0 <= g0 < s1]
            for g in done:
                mx_pass(g, 1)
                g0, n = GROUPS[g]
                if g in (E - 2, E - 1):
                    nc.vector.tensor_copy(out=y[:, g0:g0 + n], in_=accs[g][:, 0:n])
                else:
                    nc.scalar.copy(out=y[:, g0:g0 + n], in_=accs[g][:, 0:n])
            for g in done:
                if g + BANKS < len(GROUPS):
                    open_group(g + BANKS)

        def product(i, t0, t1):
            m = work.tile([P, t1 - t0], F32, name="m%d_%d" % (i, t0))
            nc.vector.tensor_tensor(
                out=m[:, 0:t1 - t0],
                in0=y[:].indirect(pos_t[i][:, t0 // 16:t1 // 16]),
                in1=gate_t[i][:, t0:t1],
                op=MULT,
            )
            return m

        def store(o, t0, t1):
            nc.sync.dma_start(out=out[:, t0:t1], in_=o[:, 0:t1 - t0])

        for t0, t1, sums in ((0, 128, (128,)), (128, 640, (512,)), (640, 1216, (320, 256))):
            m0 = product(0, t0, t1)
            m1 = product(1, t0, t1)
            c0 = t0
            for step in sums:
                total = psum.tile([P, 512], F32, name="acc")
                for i, m in enumerate((m0, m1)):
                    nc.tensor.matmul(
                        total[:, 0:step],
                        lhsT=ident[:],
                        rhs=m[:, c0 - t0:c0 - t0 + step],
                        start=(i == 0),
                        stop=(i == 1),
                    )
                o = outs.tile([P, step], F32, name="o%d" % c0)
                nc.scalar.copy(out=o[:], in_=total[:, 0:step])
                store(o, c0, c0 + step)
                c0 += step

        def vadd(ma, mb, t0, t1):
            o = outs.tile([P, t1 - t0], F32, name="o%d" % t0)
            nc.vector.tensor_tensor(out=o[:, 0:t1 - t0], in0=ma[:, 0:t1 - t0], in1=mb[:, 0:t1 - t0], op=ADD)
            store(o, t0, t1)

        a0 = product(0, 1216, 1920)
        a1 = product(1, 1216, 1920)
        b0 = product(0, 1920, 2048)
        vadd(a0, a1, 1216, 1920)
        b1 = product(1, 1920, 2048)
        vadd(b0, b1, 1920, 2048)
